import numpy as np
import ml_dtypes


def mxq(x, axis, fmt="e4m3"):
    dtype, down = {"e4m3": (ml_dtypes.float8_e4m3fn, 7), "e5m2": (ml_dtypes.float8_e5m2, 14)}[fmt]
    v = np.moveaxis(np.asarray(x, np.float32).astype(ml_dtypes.bfloat16).astype(np.float64), axis, -1)
    blocks = v.reshape(v.shape[:-1] + (-1, 32))
    amax = np.abs(blocks).max(-1, keepdims=True)
    byte = np.maximum(np.where(amax > 0, np.frexp(amax)[1] - 1 + 127, 0) - down, 1)
    scale = np.exp2(byte - 127.0)
    codes = (blocks / scale).astype(np.float32).astype(dtype).astype(np.float64)
    return np.moveaxis((codes * scale).reshape(v.shape), -1, axis)


WIDE = False


def mx_kscale(k):
    if not WIDE:
        return np.ones(k)
    levels = np.array([10, -10, 5, -5, 0])
    if k % 512:
        return np.exp2(np.random.permutation(np.resize(levels, k // 32))).repeat(32)
    a = np.empty((k // 512, 16))
    for p in range(k // 512):
        a[p, :8] = np.random.permutation(np.resize(levels, 8))
        for g in range(8):
            far = levels[np.abs(levels - a[p, g]) >= 10]
            a[p, g + 8] = far[np.random.randint(len(far))]
    return np.exp2(a.ravel()).repeat(32)


BF16 = ml_dtypes.bfloat16


def bf(x):
    return np.asarray(x, np.float32).astype(BF16)


def f64(x):
    return np.asarray(x).astype(np.float64)


E2M1 = np.array([0.0, 0.5, 1.0, 1.5, 2.0, 3.0, 4.0, 6.0, -0.0, -0.5, -1.0, -1.5, -2.0, -3.0, -4.0, -6.0])


def pack_weight(w, fmt):
    k, n = w.shape
    w = f64(bf(w)).reshape(k // 32, 32, n)
    amax = np.abs(w).max(1)
    if fmt == "e4m3":
        byte = np.frexp(amax)[1] - 1 + 127 - 7
    else:
        mant, ex = np.frexp(amax / 6.0)
        byte = np.where(mant > 0.5, ex, ex - 1) + 127
    byte = np.clip(np.where(amax > 0, byte, 1), 1, 254)
    scaled = (w * np.exp2(127.0 - byte)[:, None, :]).reshape(k, n).astype(np.float32)
    by_word = np.ascontiguousarray(scaled.reshape(k // 512, 128, 4, n).transpose(0, 1, 3, 2))
    if fmt == "e4m3":
        words = by_word.astype(ml_dtypes.float8_e4m3fn).view(np.uint8)
    else:
        c = by_word.astype(ml_dtypes.float4_e2m1fn).view(np.uint8) & 0xF
        words = c[..., 0::2] | (c[..., 1::2] << 4)
    return np.ascontiguousarray(words), np.ascontiguousarray(byte.astype(np.uint8).reshape(k // 512, 16, n))


def unpack_weight(words, scales, fmt):
    g, p, n, _ = words.shape
    if fmt == "e4m3":
        vals = np.ascontiguousarray(words).view(ml_dtypes.float8_e4m3fn).astype(np.float64)
    else:
        nib = np.empty((g, p, n, 4), np.uint8)
        nib[..., 0::2] = words & 0xF
        nib[..., 1::2] = words >> 4
        vals = E2M1[nib]
    vals = vals * np.repeat(np.exp2(scales.astype(np.float64) - 127.0), 8, axis=1)[..., None]
    return vals.transpose(0, 1, 3, 2).reshape(g * 512, n)
def pack4(w):
    words, scales = pack_weight(w, "e2m1")
    return words.reshape(words.shape[0], 128, -1), scales


def unpack4(words, scales):
    return unpack_weight(words.reshape(words.shape[0], 128, -1, 2), scales, "e2m1")


T0, T1, D, F, R = 512, 1024, 1024, 2048, 512


def draw0():
    s0, s1 = mx_kscale(T0), mx_kscale(T1)
    u = mx_kscale(F)
    x0 = np.random.standard_normal((T0, D)) * s0[:, None]
    dy0 = np.random.standard_normal((T0, F)) / np.sqrt(T0 + T1) / s0[:, None] * u
    x1 = np.random.standard_normal((T1, D)) * s1[:, None]
    dy1 = np.random.standard_normal((T1, F)) / np.sqrt(T0 + T1) / s1[:, None] * u
    basis = np.random.standard_normal((F, R)) / np.sqrt(F) / u[:, None]
    x1_words, x1_scales = pack4(x1)
    basis_words, basis_scales = pack4(basis)
    return {"x0": bf(x0), "dy0": bf(dy0),
            "x1_words": x1_words, "x1_scales": x1_scales, "dy1": bf(dy1),
            "w": bf(np.random.standard_normal((D, F))),
            "decay": bf(np.random.uniform(0.2, 0.6, F) * u),
            "basis_words": basis_words, "basis_scales": basis_scales}


def core(x0, dy0, x1_words, x1_scales, dy1, w, decay, basis_words, basis_scales):
    own = mxq(f64(x0), 0, "e4m3").T @ mxq(f64(dy0), 0, "e4m3")
    other = unpack4(x1_words, x1_scales).T @ mxq(f64(dy1), 0, "e4m3")
    g = own + other + f64(decay) * f64(w)
    return mxq(g, 1, "e4m3") @ unpack4(basis_words, basis_scales)


def e4m3fn_bytes(y):
    return np.clip(np.asarray(y, np.float64), -448.0, 448.0).astype(np.float32).astype(ml_dtypes.float8_e4m3fn).view(np.uint8)


def e4m3fn_values(b):
    return np.asarray(b, np.uint8).view(ml_dtypes.float8_e4m3fn).astype(np.float64)


def setup_inputs():
    d = draw0()
    x0 = np.asarray(d['x0']).astype(np.float64)
    s = (np.max(np.abs(x0), axis=(1,), keepdims=True) / 448.0).astype(np.float32)
    out = {}
    for k, v in d.items():
        if k == 'x0':
            out['x0_bytes'] = e4m3fn_bytes(x0 / s.astype(np.float64))
            out['x0_scale'] = s
        else:
            out[k] = v
    return out


def reference(x0_bytes, x0_scale, dy0, x1_words, x1_scales, dy1, w, decay, basis_words, basis_scales):
    return core(e4m3fn_values(x0_bytes) * x0_scale.astype(np.float64), dy0, x1_words, x1_scales, dy1, w, decay, basis_words, basis_scales)

@@ -1,0 +1,314 @@
+from contextlib import ExitStack
+
+import concourse.mybir as mybir
+from concourse.masks import make_identity
+
+T0, T1, D, F, R = 512, 1024, 1024, 2048, 512
+FLOPS = 2 * D * F * (T0 + T1) + 2 * D * F * R
+
+F32 = mybir.dt.float32
+BF16 = mybir.dt.bfloat16
+U32 = mybir.dt.uint32
+I32 = mybir.dt.int32
+U8 = mybir.dt.uint8
+FP8 = mybir.dt.float8_e4m3fn
+FP8X4 = mybir.dt.float8_e4m3fn_x4
+FP4X4 = mybir.dt.float4_e2m1fn_x4
+COPY = mybir.ActivationFunctionType.Copy
+ADD = mybir.AluOpType.add
+MULT = mybir.AluOpType.mult
+
+P = 128
+K = 512
+NJ = (T0 + T1) // K
+NG = F // K
+ND = D // P
+
+
+def tile_replica_weight_gradient_sketch_s3_kernel(
+    tc, x0_bytes, x0_scale, dy0, x1_words, x1_scales, dy1, w, decay, basis_words, basis_scales, out
+):
+    nc = tc.nc
+    with ExitStack() as ctx:
+        keep = ctx.enter_context(tc.tile_pool(name="keep", bufs=1))
+        work = ctx.enter_context(tc.tile_pool(name="work", bufs=2))
+        psum = ctx.enter_context(tc.psum_pool(name="psum", bufs=1))
+        ctx.enter_context(tc.manual_schedule())
+
+        def sb(name, shape, dtype):
+            return keep.tile(shape, dtype, name=name, align_bytes=64)
+
+        x0_raw = [sb("x0_raw%d" % h, [P, 4, 512], U8) for h in range(2)]
+        x0_sc = sb("x0_sc", [P, 4], F32)
+        x0_wide = [sb("x0_wide%d" % h, [P, 4, 512], BF16) for h in range(2)]
+        x0_int = sb("x0_int", [P, D, 4], BF16)
+        x0_q = sb("x0_q", [P, D], U32)
+        x0_s = sb("x0_s", [P, D], U8)
+        x1_w = [sb("x1_w%d" % h, [P, 2, D], U8) for h in range(2)]
+        x1_s = sb("x1_s", [P, 2, D], U8)
+        b_w = sb("b_w", [P, NG, 2 * R], U8)
+        b_s = sb("b_s", [P, NG, R], U8)
+        dy_raw, w_sb = {}, {}
+        for g, n in ((0, 1), (1, 1), (2, 2)):
+            for j in range(NJ):
+                tile = sb("dy_raw_%d_%d" % (j, g), [P, 4, n * K], BF16)
+                for k in range(n):
+                    dy_raw[j, g + k] = tile[:, :, K * k : K * (k + 1)]
+                dy_raw[j, g, "all"] = tile
+            for h in range(2):
+                tile = sb("w_sb_%d_%d" % (h, g), [P, 4, n * K], BF16)
+                for k in range(n):
+                    for i in range(4):
+                        w_sb[4 * h + i, g + k] = tile[:, i, K * k : K * (k + 1)]
+                w_sb[h, g, "all"] = tile
+        dec_b = sb("dec_b", [P, NG, 4], BF16)
+        dec = sb("dec", [P, NG, 4], F32)
+        ident = sb("ident", [P, P], F32)
+        warm = sb("warm", [P, 1], F32)
+        g_q = [sb("g_q%d" % g, [P, D], U32) for g in range(NG)]
+        g_s = [sb("g_s%d" % g, [P, D], U8) for g in range(NG)]
+
+        x0_rows = x0_bytes.rearrange("(p s) d -> p s d", s=4)
+        dy_rows = [dy0.rearrange("(p s) f -> p s f", s=4)] + [
+            dy1[K * j : K * (j + 1), :].rearrange("(p s) f -> p s f", s=4) for j in range(2)
+        ]
+        w_rows = w.rearrange("(i p) f -> p i f", p=P)
+        x1_cols = x1_words.rearrange("g p n -> p g n")
+
+        def load_x0(h):
+            c = slice(512 * h, 512 * (h + 1))
+            nc.sync.dma_start(out=x0_raw[h][:], in_=x0_rows[:, :, c])
+
+        def load_x1(h):
+            c = slice(1024 * h, 1024 * (h + 1))
+            nc.sync.dma_start(out=x1_w[h][:], in_=x1_cols[:, :, c])
+
+        def load_dy(j, g, n=1):
+            c = slice(K * g, K * (g + n))
+            nc.sync.dma_start(out=dy_raw[j, g, "all"][:], in_=dy_rows[j][:, :, c])
+
+        def load_w(h, g, n=1):
+            c = slice(K * g, K * (g + n))
+            nc.sync.dma_start(out=w_sb[h, g, "all"][:], in_=w_rows[:, 4 * h : 4 * (h + 1), c])
+
+        def load_scales(tile, dram):
+            for q in range(4):
+                nc.sync.dma_start(
+                    out=tile[32 * q : 32 * q + 4, :, :].bitcast(I32),
+                    in_=dram[:, 4 * q : 4 * q + 4, :].rearrange("g q n -> q g n").bitcast(I32),
+                )
+
+        nc.scalar.dma_start(out=x0_sc[:], in_=x0_scale.rearrange("(p s) o -> p (s o)", s=4))
+        nc.scalar.dma_start(out=dec_b[:], in_=decay.rearrange("(g p t) -> p g t", p=P, t=4))
+        nc.gpsimd.memset(x1_s[:].rearrange("p g n -> p (g n)").bitcast(I32), 0)
+        nc.gpsimd.memset(b_s[:].rearrange("p g n -> p (g n)").bitcast(I32), 0)
+        make_identity(nc, ident[:])
+        nc.vector.memset(warm[:], 0.0)
+        nc.scalar.activation(out=warm[:], in_=warm[:], func=COPY, scale=1.0)
+
+        load_x0(0)
+        load_dy(0, 0)
+        load_dy(1, 0)
+        load_dy(2, 0)
+        load_w(0, 0)
+        load_x1(0)
+        load_scales(x1_s, x1_scales)
+        load_x0(1)
+        load_x1(1)
+        load_w(1, 0)
+        for j in range(NJ):
+            load_dy(j, 1)
+        nc.sync.dma_start(out=b_w[:], in_=basis_words.rearrange("g p n -> p g n"))
+        load_scales(b_s, basis_scales)
+        load_w(0, 1)
+        load_w(1, 1)
+        for j in range(NJ):
+            load_dy(j, 2, 2)
+        load_w(0, 2, 2)
+        load_w(1, 2, 2)
+
+        dy_int, dy_q, dy_s = {}, {}, {}
+
+        def copy_on(engine, dst, src):
+            if engine == "v":
+                nc.vector.tensor_copy(out=dst, in_=src)
+            else:
+                nc.scalar.copy(out=dst, in_=src)
+
+        def x0_widen(h, s):
+            nc.vector.tensor_scalar(
+                out=x0_wide[h][:, s, :], in0=x0_raw[h][:, s, :].bitcast(FP8), scalar1=x0_sc[:, s : s + 1], scalar2=None, op0=MULT
+            )
+
+        def x0_interleave(engine, h, c0, n):
+            copy_on(
+                engine,
+                x0_int[:, 512 * h + c0 : 512 * h + c0 + n, :].rearrange("p (b i) s -> p b s i", i=4),
+                x0_wide[h][:, :, c0 : c0 + n].rearrange("p s (b i) -> p b s i", i=4),
+            )
+
+        def x0_quant(h):
+            c = slice(512 * h, 512 * (h + 1))
+            nc.vector.quantize_mx(
+                out=x0_q[:, c].bitcast(FP8X4), scales=x0_s[:, c], in_=x0_int[:, c, :].rearrange("p d s -> p (d s)")
+            )
+
+        def dy_interleave(engine, j, g, t):
+            if (j, g) not in dy_int:
+                dy_int[j, g] = work.tile([P, 4, P, 4], BF16, name="dy_int", bufs=3, align_bytes=64)
+            copy_on(
+                engine,
+                dy_int[j, g][:, t, :, :].rearrange("p (b i) s -> p b s i", i=2),
+                dy_raw[j, g].rearrange("p s (b i t) -> p t b s i", i=2, t=4)[:, t],
+            )
+
+        def dy_quant(j, g):
+            dy_q[j, g] = work.tile([P, K], U32, name="dy_q%d" % j, align_bytes=64)
+            dy_s[j, g] = work.tile([P, K], U8, name="dy_s%d" % j, align_bytes=64)
+            nc.vector.quantize_mx(
+                out=dy_q[j, g][:].bitcast(FP8X4),
+                scales=dy_s[j, g][:],
+                in_=dy_int[j, g][:].rearrange("p t m s -> p (t m s)"),
+            )
+
+        wt, dw, acc, g_ps, g_in = {}, {}, {}, {}, {}
+
+        def w_transpose(g, ip, bank):
+            wt[g, ip] = psum.tile([P, 2, 256], F32, name=bank)
+            for half in range(2):
+                words = w_sb[2 * ip + half, g].bitcast(F32)
+                for u in range(2):
+                    nc.tensor.transpose(
+                        wt[g, ip][:, u, P * half : P * (half + 1)], words[:, u::2], ident[:]
+                    )
+
+        def decay_times_w(g, ip):
+            dw[g, ip] = work.tile([P, 4, 256], F32, name="dw", bufs=5, align_bytes=64)
+            for t in range(4):
+                nc.scalar.activation(
+                    out=dw[g, ip][:, t, :],
+                    in_=wt[g, ip][:, t // 2, :].bitcast(BF16).rearrange("p (d e) -> p e d", e=2)[:, t % 2, :],
+                    func=COPY,
+                    scale=dec[:, g, t : t + 1],
+                )
+
+        def gradient(g, i):
+            g_ps[g, i] = psum.tile([P, 4, P], F32, name="bank_g%d" % (i % 2))
+            for t in range(4):
+                for j in range(NJ):
+                    m = slice(P * t, P * (t + 1))
+                    d = slice(P * i, P * (i + 1))
+                    if j == 0:
+                        rhs, rhs_scale = x0_q[:, d].bitcast(FP8X4), x0_s[:, d]
+                    else:
+                        rhs = x1_w[i // 4][:, j - 1, 2 * P * (i % 4) : 2 * P * (i % 4 + 1)].bitcast(FP4X4)
+                        rhs_scale = x1_s[:, j - 1, d]
+                    nc.tensor.matmul_mx(
+                        out=g_ps[g, i][:, t, :],
+                        lhsT=dy_q[j, g][:, m].bitcast(FP8X4),
+                        lhsT_scale=dy_s[j, g][:, m],
+                        rhs=rhs,
+                        rhs_scale=rhs_scale,
+                        start=(j == 0),
+                        stop=(j == NJ - 1),
+                    )
+
+        def add_decay(g, i):
+            g_in[g, i] = work.tile([P, P, 4], BF16, name="g_in", bufs=4, align_bytes=64)
+            half = slice(P * (i % 2), P * (i % 2 + 1))
+            nc.vector.tensor_tensor(
+                out=g_in[g, i][:].rearrange("p (b i) t -> p b t i", i=2),
+                in0=g_ps[g, i][:].rearrange("p t (b i) -> p b t i", i=2),
+                in1=dw[g, i // 2][:, :, half].rearrange("p t (b i) -> p b t i", i=2),
+                op=ADD,
+            )
+
+        def g_quant(g, i):
+            d = slice(P * i, P * (i + 1))
+            nc.vector.quantize_mx(
+                out=g_q[g][:, d].bitcast(FP8X4), scales=g_s[g][:, d], in_=g_in[g, i][:].rearrange("p d t -> p (d t)")
+            )
+
+        def project(g, i, bank):
+            if i not in acc:
+                acc[i] = psum.tile([P, R], F32, name=bank)
+            d = slice(P * i, P * (i + 1))
+            nc.tensor.matmul_mx(
+                out=acc[i][:],
+                lhsT=g_q[g][:, d].bitcast(FP8X4),
+                lhsT_scale=g_s[g][:, d],
+                rhs=b_w[:, g, :].bitcast(FP4X4),
+                rhs_scale=b_s[:, g, :],
+                start=(g == 0),
+                stop=(g == NG - 1),
+            )
+
+        def store(engine, i):
+            res = work.tile([P, R], F32, name="res", bufs=3, align_bytes=64)
+            copy_on(engine, res[:], acc[i][:])
+            nc.sync.dma_start(out=out[P * i : P * (i + 1), :], in_=res[:])
+
+        for s in range(4):
+            x0_widen(0, s)
+        x0_interleave("v", 0, 0, 512)
+        for t in range(4):
+            dy_interleave("s", 0, 0, t)
+        for t in range(4):
+            dy_interleave("v", 1, 0, t)
+        x0_quant(0)
+        for t in range(4):
+            dy_interleave("s" if t < 2 else "v", 2, 0, t)
+        nc.vector.tensor_copy(out=dec[:], in_=dec_b[:])
+        dy_quant(0, 0)
+        dy_quant(1, 0)
+        dy_quant(2, 0)
+        w_transpose(0, 0, "bank_w0")
+        w_transpose(0, 1, "bank_w1")
+        decay_times_w(0, 0)
+
+        units = [(g, i) for g in range(NG) for i in range(ND)]
+        late_bank = {i: "bank_a%d" % (i - 4) for i in range(4, ND)}
+        last = NG - 1
+
+        def project_next(n):
+            g, i = units[n]
+            if i < 4:
+                for pg in {0: (), 1: (0, 1)}.get(g, (g,)):
+                    project(pg, i, "bank_a%d" % i)
+            elif g == last:
+                project(g, i, late_bank[i])
+            if g == last:
+                store("s" if i < ND - 1 else "v", i)
+
+        for n, (g, i) in enumerate(units):
+            gradient(g, i)
+            if n % 4 == 1 and n // 2 + 3 < 4 * NG:
+                for q in (n // 2 + 2, n // 2 + 3):
+                    w_transpose(q // 4, q % 4, "bank_w%d" % (q % 2))
+            if n % 2 == 0 and n // 2 + 1 < 4 * NG:
+                decay_times_w((n // 2 + 1) // 4, (n // 2 + 1) % 4)
+            if g == 0 and i < 2:
+                for s in (2 * i, 2 * i + 1):
+                    x0_widen(1, s)
+            if g < last and i in (2, 4, 6):
+                dy_quant(i // 2 - 1, g + 1)
+            add_decay(g, i)
+            if n > 0:
+                g_quant(*units[n - 1])
+            if n > 1:
+                project_next(n - 2)
+            if g == last and 3 <= i < 7:
+                for pg in range(last):
+                    project(pg, i + 1, late_bank[i + 1])
+            if g == 0 and i == 1:
+                x0_interleave("s", 1, 0, 256)
+                x0_interleave("v", 1, 256, 256)
+            if g == 0 and i == 2:
+                x0_quant(1)
+            if g < last:
+                if i < 6:
+                    for t in (2 * (i % 2), 2 * (i % 2) + 1):
+                        dy_interleave("s" if t % 2 == 0 else "v", i // 2, g + 1, t)
+        project_next(len(units) - 2)
+        g_quant(*units[-1])
+        project_next(len(units) - 1)

@@ -118,9 +118,9 @@ def tile_replica_weight_gradient_sketch_s3_kernel(
         load_w(1, 0)
         for j in range(NJ):
             load_dy(j, 1)
+        load_w(0, 1)
         nc.sync.dma_start(out=b_w[:], in_=basis_words.rearrange("g p n -> p g n"))
         load_scales(b_s, basis_scales)
-        load_w(0, 1)
         load_w(1, 1)
         for j in range(NJ):
             load_dy(j, 2, 2)
@@ -135,20 +135,22 @@ def tile_replica_weight_gradient_sketch_s3_kernel(
             else:
                 nc.scalar.copy(out=dst, in_=src)
 
-        def x0_widen(h, s):
-            nc.vector.tensor_scalar(
-                out=x0_wide[h][:, s, :], in0=x0_raw[h][:, s, :].bitcast(FP8), scalar1=x0_sc[:, s : s + 1], scalar2=None, op0=MULT
-            )
+        def x0_widen(engine, h, s):
+            dst, src = x0_wide[h][:, s, :], x0_raw[h][:, s, :].bitcast(FP8)
+            if engine == "v":
+                nc.vector.tensor_scalar(out=dst, in0=src, scalar1=x0_sc[:, s : s + 1], scalar2=None, op0=MULT)
+            else:
+                nc.scalar.activation(out=dst, in_=src, func=COPY, scale=x0_sc[:, s : s + 1])
 
-        def x0_interleave(engine, h, c0, n):
+        def x0_interleave(engine, c):
             copy_on(
                 engine,
-                x0_int[:, 512 * h + c0 : 512 * h + c0 + n, :].rearrange("p (b i) s -> p b s i", i=4),
-                x0_wide[h][:, :, c0 : c0 + n].rearrange("p s (b i) -> p b s i", i=4),
+                x0_int[:, 256 * c : 256 * (c + 1), :].rearrange("p (b i) s -> p b s i", i=4),
+                x0_wide[c // 2][:, :, 256 * (c % 2) : 256 * (c % 2 + 1)].rearrange("p s (b i) -> p b s i", i=4),
             )
 
-        def x0_quant(h):
-            c = slice(512 * h, 512 * (h + 1))
+        def x0_quant(c):
+            c = slice(256 * c, 256 * (c + 1))
             nc.vector.quantize_mx(
                 out=x0_q[:, c].bitcast(FP8X4), scales=x0_s[:, c], in_=x0_int[:, c, :].rearrange("p d s -> p (d s)")
             )
@@ -192,8 +194,8 @@ def tile_replica_weight_gradient_sketch_s3_kernel(
                     scale=dec[:, g, t : t + 1],
                 )
 
-        def gradient(g, i):
-            g_ps[g, i] = psum.tile([P, 4, P], F32, name="bank_g%d" % (i % 2))
+        def gradient(g, i, bank):
+            g_ps[g, i] = psum.tile([P, 4, P], F32, name="bank_" + bank)
             for t in range(4):
                 for j in range(NJ):
                     m = slice(P * t, P * (t + 1))
@@ -244,71 +246,88 @@ def tile_replica_weight_gradient_sketch_s3_kernel(
             )
 
         def store(engine, i):
-            res = work.tile([P, R], F32, name="res", bufs=3, align_bytes=64)
+            res = work.tile([P, R], F32, name="res", bufs=6, align_bytes=64)
             copy_on(engine, res[:], acc[i][:])
             nc.sync.dma_start(out=out[P * i : P * (i + 1), :], in_=res[:])
 
         for s in range(4):
-            x0_widen(0, s)
-        x0_interleave("v", 0, 0, 512)
+            x0_widen("s" if s == 3 else "v", 0, s)
+        x0_interleave("v", 0)
         for t in range(4):
             dy_interleave("s", 0, 0, t)
         for t in range(4):
-            dy_interleave("v", 1, 0, t)
+            dy_interleave("s" if t == 0 else "v", 1, 0, t)
         x0_quant(0)
         for t in range(4):
             dy_interleave("s" if t < 2 else "v", 2, 0, t)
-        nc.vector.tensor_copy(out=dec[:], in_=dec_b[:])
         dy_quant(0, 0)
+        nc.vector.tensor_copy(out=dec[:], in_=dec_b[:])
         dy_quant(1, 0)
         dy_quant(2, 0)
         w_transpose(0, 0, "bank_w0")
         w_transpose(0, 1, "bank_w1")
         decay_times_w(0, 0)
+        for s in range(4):
+            x0_widen("s", 1, s)
+        decay_times_w(0, 1)
 
         units = [(g, i) for g in range(NG) for i in range(ND)]
-        late_bank = {i: "bank_a%d" % (i - 4) for i in range(4, ND)}
         last = NG - 1
 
-        def project_next(n):
-            g, i = units[n]
-            if i < 4:
-                for pg in {0: (), 1: (0, 1)}.get(g, (g,)):
-                    project(pg, i, "bank_a%d" % i)
-            elif g == last:
-                project(g, i, late_bank[i])
-            if g == last:
-                store("s" if i < ND - 1 else "v", i)
+        def prepare(g, i):
+            if g == 0:
+                if i == 0:
+                    x0_interleave("v", 1)
+                elif i == 1:
+                    x0_quant(1)
+                elif i == 2:
+                    x0_interleave("v", 2)
+                elif i == 3:
+                    x0_quant(2)
+                    x0_interleave("v", 3)
+                elif i == 4:
+                    x0_quant(3)
+            if g < last:
+                for k in range(12):
+                    j, t = divmod(k, 4)
+                    if g == 0 and k * 2 // 3 == i or g > 0 and k // 2 == i:
+                        dy_interleave("s" if (t < (3 if j < 1 else 2) if g == 0 else t % 2 == 0) else "v", j, g + 1, t)
+                if g == 0:
+                    if i in (4, 6, 7):
+                        dy_quant({4: 0, 6: 1, 7: 2}[i], 1)
+                elif i in (2, 4, 6):
+                    dy_quant(i // 2 - 1, g + 1)
 
         for n, (g, i) in enumerate(units):
-            gradient(g, i)
-            if n % 4 == 1 and n // 2 + 3 < 4 * NG:
+            gradient(g, i, "g%d" % (n % 2) if n >= 6 else ("g0", "g1", "a2", "a3")[n % 4])
+            if n == 1:
+                w_transpose(0, 2, "bank_a0")
+                w_transpose(0, 3, "bank_a1")
+            elif n == 5:
+                w_transpose(1, 0, "bank_w0")
+                w_transpose(1, 1, "bank_w1")
+            elif n == 8:
+                w_transpose(1, 2, "bank_a0")
+                w_transpose(1, 3, "bank_a1")
+            elif n > 9 and n % 4 == 0 and n < 27:
                 for q in (n // 2 + 2, n // 2 + 3):
                     w_transpose(q // 4, q % 4, "bank_w%d" % (q % 2))
-            if n % 2 == 0 and n // 2 + 1 < 4 * NG:
-                decay_times_w((n // 2 + 1) // 4, (n // 2 + 1) % 4)
-            if g == 0 and i < 2:
-                for s in (2 * i, 2 * i + 1):
-                    x0_widen(1, s)
-            if g < last and i in (2, 4, 6):
-                dy_quant(i // 2 - 1, g + 1)
+            q = (n + 3) // 2
+            if n % 2 == 1 and q < 4 * NG:
+                decay_times_w(q // 4, q % 4)
+            prepare(g, i)
             add_decay(g, i)
             if n > 0:
                 g_quant(*units[n - 1])
             if n > 1:
-                project_next(n - 2)
-            if g == last and 3 <= i < 7:
-                for pg in range(last):
-                    project(pg, i + 1, late_bank[i + 1])
-            if g == 0 and i == 1:
-                x0_interleave("s", 1, 0, 256)
-                x0_interleave("v", 1, 256, 256)
-            if g == 0 and i == 2:
-                x0_quant(1)
-            if g < last:
-                if i < 6:
-                    for t in (2 * (i % 2), 2 * (i % 2) + 1):
-                        dy_interleave("s" if t % 2 == 0 else "v", i // 2, g + 1, t)
-        project_next(len(units) - 2)
+                pg, pi = units[n - 2]
+                if pi < 4 and pg > 0:
+                    for h in range(0 if pg == 1 else pg, pg + 1):
+                        project(h, pi, "bank_a%d" % pi)
+                    if pg == last:
+                        store("s", pi)
         g_quant(*units[-1])
-        project_next(len(units) - 1)
+        for i in range(4, ND):
+            for g in range(NG):
+                project(g, i, "bank_a%d" % (i - 4))
+            store("s" if i % 2 == 0 else "v", i)

@@ -18,6 +18,7 @@ COPY = mybir.ActivationFunctionType.Copy
 ADD = mybir.AluOpType.add
 MULT = mybir.AluOpType.mult
 
+PQ, NS, LAG = 8, 3, 3
 P = 128
 K = 512
 NJ = (T0 + T1) // K
@@ -49,7 +50,7 @@ def tile_replica_weight_gradient_sketch_s3_kernel(
         b_w = sb("b_w", [P, NG, 2 * R], U8)
         b_s = sb("b_s", [P, NG, R], U8)
         dy_raw, w_sb = {}, {}
-        for g, n in ((0, 1), (1, 1), (2, 2)):
+        for g, n in ((0, 1), (1, 1), (2, 1), (3, 1)):
             for j in range(NJ):
                 tile = sb("dy_raw_%d_%d" % (j, g), [P, 4, n * K], BF16)
                 for k in range(n):
@@ -64,6 +65,7 @@ def tile_replica_weight_gradient_sketch_s3_kernel(
         dec_b = sb("dec_b", [P, NG, 4], BF16)
         dec = sb("dec", [P, NG, 4], F32)
         ident = sb("ident", [P, P], F32)
+        ident_b = sb("ident_b", [P, P], BF16)
         warm = sb("warm", [P, 1], F32)
         g_q = [sb("g_q%d" % g, [P, D], U32) for g in range(NG)]
         g_s = [sb("g_s%d" % g, [P, D], U8) for g in range(NG)]
@@ -100,6 +102,7 @@ def tile_replica_weight_gradient_sketch_s3_kernel(
 
         nc.scalar.dma_start(out=x0_sc[:], in_=x0_scale.rearrange("(p s) o -> p (s o)", s=4))
         nc.scalar.dma_start(out=dec_b[:], in_=decay.rearrange("(g p t) -> p g t", p=P, t=4))
+        make_identity(nc, ident_b[:])
         nc.gpsimd.memset(x1_s[:].rearrange("p g n -> p (g n)").bitcast(I32), 0)
         nc.gpsimd.memset(b_s[:].rearrange("p g n -> p (g n)").bitcast(I32), 0)
         make_identity(nc, ident[:])
@@ -114,18 +117,20 @@ def tile_replica_weight_gradient_sketch_s3_kernel(
         load_x1(0)
         load_scales(x1_s, x1_scales)
         load_x0(1)
-        load_x1(1)
         load_w(1, 0)
+        load_x1(1)
         for j in range(NJ):
             load_dy(j, 1)
         load_w(0, 1)
         nc.sync.dma_start(out=b_w[:], in_=basis_words.rearrange("g p n -> p g n"))
         load_scales(b_s, basis_scales)
         load_w(1, 1)
-        for j in range(NJ):
-            load_dy(j, 2, 2)
-        load_w(0, 2, 2)
-        load_w(1, 2, 2)
+        for g in (2, 3):
+            load_dy(0, g)
+            load_dy(1, g)
+            load_w(0, g)
+            load_dy(2, g)
+            load_w(1, g)
 
         dy_int, dy_q, dy_s = {}, {}, {}
 
@@ -164,25 +169,50 @@ def tile_replica_weight_gradient_sketch_s3_kernel(
                 dy_raw[j, g].rearrange("p s (b i t) -> p t b s i", i=2, t=4)[:, t],
             )
 
-        def dy_quant(j, g):
-            dy_q[j, g] = work.tile([P, K], U32, name="dy_q%d" % j, align_bytes=64)
-            dy_s[j, g] = work.tile([P, K], U8, name="dy_s%d" % j, align_bytes=64)
+        def dy_interleave_by_matmul(j, g, bank, t0):
+            if (j, g) not in dy_int:
+                dy_int[j, g] = work.tile([P, 4, P, 4], BF16, name="dy_int", bufs=3, align_bytes=64)
+            moved = psum.tile([P, 2, P, 4], BF16, name=bank)
+            for k in range(2):
+                nc.tensor.matmul(
+                    out=moved[:, k, :, :],
+                    lhsT=ident_b[:],
+                    rhs=dy_raw[j, g].rearrange("p s (m t) -> p t m s", t=4)[:, t0 + k],
+                    start=True,
+                    stop=True,
+                )
+            nc.scalar.copy(out=dy_int[j, g][:, t0 : t0 + 2, :, :], in_=moved[:])
+
+        def dy_quant(j, g, t0=0, n=4):
+            if t0 == 0:
+                dy_q[j, g] = work.tile([P, K], U32, name="dy_q%d" % j, align_bytes=64)
+                dy_s[j, g] = work.tile([P, K], U8, name="dy_s%d" % j, align_bytes=64)
+            c = slice(P * t0, P * (t0 + n))
             nc.vector.quantize_mx(
-                out=dy_q[j, g][:].bitcast(FP8X4),
-                scales=dy_s[j, g][:],
-                in_=dy_int[j, g][:].rearrange("p t m s -> p (t m s)"),
+                out=dy_q[j, g][:, c].bitcast(FP8X4),
+                scales=dy_s[j, g][:, c],
+                in_=dy_int[j, g][:, t0 : t0 + n, :, :].rearrange("p t m s -> p (t m s)"),
             )
 
         wt, dw, acc, g_ps, g_in = {}, {}, {}, {}, {}
+
+        w_perm = {}
+
+        def w_permute(g, ip):
+            w_perm[g, ip] = work.tile([P, 2, 2, P], F32, name="w_perm", bufs=4, align_bytes=64)
+            for half in range(2):
+                nc.vector.tensor_copy(
+                    out=w_perm[g, ip][:, half, :, :],
+                    in_=w_sb[2 * ip + half, g].bitcast(F32).rearrange("p (m u) -> p u m", u=2),
+                )
 
         def w_transpose(g, ip, bank):
             wt[g, ip] = psum.tile([P, 2, 256], F32, name=bank)
             for half in range(2):
                 words = w_sb[2 * ip + half, g].bitcast(F32)
                 for u in range(2):
-                    nc.tensor.transpose(
-                        wt[g, ip][:, u, P * half : P * (half + 1)], words[:, u::2], ident[:]
-                    )
+                    src = w_perm[g, ip][:, half, u, :] if (g, ip) in w_perm else words[:, u::2]
+                    nc.tensor.transpose(wt[g, ip][:, u, P * half : P * (half + 1)], src, ident[:])
 
         def decay_times_w(g, ip):
             dw[g, ip] = work.tile([P, 4, 256], F32, name="dw", bufs=5, align_bytes=64)
@@ -216,7 +246,10 @@ def tile_replica_weight_gradient_sketch_s3_kernel(
                     )
 
         def add_decay(g, i):
-            g_in[g, i] = work.tile([P, P, 4], BF16, name="g_in", bufs=4, align_bytes=64)
+            if g == 0:
+                g_in[g, i] = work.tile([P, P, 4], BF16, name="g_in0", bufs=ND, align_bytes=64)
+            else:
+                g_in[g, i] = work.tile([P, P, 4], BF16, name="g_in", bufs=4, align_bytes=64)
             half = slice(P * (i % 2), P * (i % 2 + 1))
             nc.vector.tensor_tensor(
                 out=g_in[g, i][:].rearrange("p (b i) t -> p b t i", i=2),
@@ -245,25 +278,28 @@ def tile_replica_weight_gradient_sketch_s3_kernel(
                 stop=(g == NG - 1),
             )
 
-        def store(engine, i):
+        def store(engine, i, pieces=1):
             res = work.tile([P, R], F32, name="res", bufs=6, align_bytes=64)
-            copy_on(engine, res[:], acc[i][:])
-            nc.sync.dma_start(out=out[P * i : P * (i + 1), :], in_=res[:])
+            for k in range(pieces):
+                c = slice(R * k // pieces, R * (k + 1) // pieces)
+                copy_on(engine, res[:, c], acc[i][:, c])
+                nc.sync.dma_start(out=out[P * i : P * (i + 1), c], in_=res[:, c])
 
         for s in range(4):
-            x0_widen("s" if s == 3 else "v", 0, s)
+            x0_widen("s" if s > 1 else "v", 0, s)
         x0_interleave("v", 0)
-        for t in range(4):
-            dy_interleave("s", 0, 0, t)
+        dy_interleave_by_matmul(0, 0, "bank_a2", 0)
         for t in range(4):
             dy_interleave("s" if t == 0 else "v", 1, 0, t)
+        dy_interleave_by_matmul(0, 0, "bank_a3", 2)
         x0_quant(0)
         for t in range(4):
             dy_interleave("s" if t < 2 else "v", 2, 0, t)
         dy_quant(0, 0)
         nc.vector.tensor_copy(out=dec[:], in_=dec_b[:])
         dy_quant(1, 0)
-        dy_quant(2, 0)
+        dy_quant(2, 0, 0, 2)
+        dy_quant(2, 0, 2, 2)
         w_transpose(0, 0, "bank_w0")
         w_transpose(0, 1, "bank_w1")
         decay_times_w(0, 0)
@@ -291,7 +327,7 @@ def tile_replica_weight_gradient_sketch_s3_kernel(
                 for k in range(12):
                     j, t = divmod(k, 4)
                     if g == 0 and k * 2 // 3 == i or g > 0 and k // 2 == i:
-                        dy_interleave("s" if (t < (3 if j < 1 else 2) if g == 0 else t % 2 == 0) else "v", j, g + 1, t)
+                        dy_interleave("s" if (t < (3 if j < 1 else 2) if g == 0 else t % 2 == 0 or t == 1 and j < NS) else "v", j, g + 1, t)
                 if g == 0:
                     if i in (4, 6, 7):
                         dy_quant({4: 0, 6: 1, 7: 2}[i], 1)
@@ -309,18 +345,25 @@ def tile_replica_weight_gradient_sketch_s3_kernel(
             elif n == 8:
                 w_transpose(1, 2, "bank_a0")
                 w_transpose(1, 3, "bank_a1")
-            elif n > 9 and n % 4 == 0 and n < 27:
+            if n % 4 >= 2 and PQ <= n // 4 * 2 + 2 + n % 4 < 16:
+                q = n // 4 * 2 + 2 + n % 4
+                w_permute(q // 4, q % 4)
+            if n > 9 and n % 4 == 0 and n < 27:
                 for q in (n // 2 + 2, n // 2 + 3):
                     w_transpose(q // 4, q % 4, "bank_w%d" % (q % 2))
-            q = (n + 3) // 2
-            if n % 2 == 1 and q < 4 * NG:
-                decay_times_w(q // 4, q % 4)
             prepare(g, i)
+            for q in range(2, 4 * NG):
+                if n == {4: 6, 5: 8}.get(q, 2 * q - 3):
+                    decay_times_w(q // 4, q % 4)
             add_decay(g, i)
-            if n > 0:
+            if n > ND:
                 g_quant(*units[n - 1])
-            if n > 1:
-                pg, pi = units[n - 2]
+            if g == 1 and i < 4:
+                g_quant(0, i)
+            if g == last and i < 4:
+                g_quant(0, i + 4)
+            if n > LAG - 1:
+                pg, pi = units[n - LAG]
                 if pi < 4 and pg > 0:
                     for h in range(0 if pg == 1 else pg, pg + 1):
                         project(h, pi, "bank_a%d" % pi)
@@ -330,4 +373,4 @@ def tile_replica_weight_gradient_sketch_s3_kernel(
         for i in range(4, ND):
             for g in range(NG):
                 project(g, i, "bank_a%d" % (i - 4))
-            store("s" if i % 2 == 0 else "v", i)
+            store("s" if i % 2 == 0 else "v", i, 2 if i == ND - 1 else 1)

@@ -18,7 +18,7 @@ COPY = mybir.ActivationFunctionType.Copy
 ADD = mybir.AluOpType.add
 MULT = mybir.AluOpType.mult
 
-PQ, NS, LAG = 8, 3, 3
+PQ, NS, LAG, EARLY, WARM, HS, H0, H1, WE = 8, 3, 3, 3, 5, 1, 4, 2, "v"
 P = 128
 K = 512
 NJ = (T0 + T1) // K
@@ -62,7 +62,7 @@ def tile_replica_weight_gradient_sketch_s3_kernel(
                     for i in range(4):
                         w_sb[4 * h + i, g + k] = tile[:, i, K * k : K * (k + 1)]
                 w_sb[h, g, "all"] = tile
-        dec_b = sb("dec_b", [P, NG, 4], BF16)
+        dec_rows = sb("dec_rows", [P, K], BF16)
         dec = sb("dec", [P, NG, 4], F32)
         ident = sb("ident", [P, P], F32)
         ident_b = sb("ident_b", [P, P], BF16)
@@ -101,9 +101,9 @@ def tile_replica_weight_gradient_sketch_s3_kernel(
                 )
 
         nc.scalar.dma_start(out=x0_sc[:], in_=x0_scale.rearrange("(p s) o -> p (s o)", s=4))
-        nc.scalar.dma_start(out=dec_b[:], in_=decay.rearrange("(g p t) -> p g t", p=P, t=4))
+        nc.vector.memset(x1_s[:].rearrange("p g n -> p (g n)").bitcast(I32), 0)
+        nc.vector.memset(dec_rows[:], 0.0)
         make_identity(nc, ident_b[:])
-        nc.gpsimd.memset(x1_s[:].rearrange("p g n -> p (g n)").bitcast(I32), 0)
         nc.gpsimd.memset(b_s[:].rearrange("p g n -> p (g n)").bitcast(I32), 0)
         make_identity(nc, ident[:])
         nc.vector.memset(warm[:], 0.0)
@@ -111,11 +111,12 @@ def tile_replica_weight_gradient_sketch_s3_kernel(
 
         load_x0(0)
         load_dy(0, 0)
+        nc.scalar.dma_start(out=dec_rows[0:NG, :], in_=decay.rearrange("(g k) -> g k", k=K))
         load_dy(1, 0)
         load_dy(2, 0)
+        load_scales(x1_s, x1_scales)
         load_w(0, 0)
         load_x1(0)
-        load_scales(x1_s, x1_scales)
         load_x0(1)
         load_w(1, 0)
         load_x1(1)
@@ -168,20 +169,6 @@ def tile_replica_weight_gradient_sketch_s3_kernel(
                 dy_int[j, g][:, t, :, :].rearrange("p (b i) s -> p b s i", i=2),
                 dy_raw[j, g].rearrange("p s (b i t) -> p t b s i", i=2, t=4)[:, t],
             )
-
-        def dy_interleave_by_matmul(j, g, bank, t0):
-            if (j, g) not in dy_int:
-                dy_int[j, g] = work.tile([P, 4, P, 4], BF16, name="dy_int", bufs=3, align_bytes=64)
-            moved = psum.tile([P, 2, P, 4], BF16, name=bank)
-            for k in range(2):
-                nc.tensor.matmul(
-                    out=moved[:, k, :, :],
-                    lhsT=ident_b[:],
-                    rhs=dy_raw[j, g].rearrange("p s (m t) -> p t m s", t=4)[:, t0 + k],
-                    start=True,
-                    stop=True,
-                )
-            nc.scalar.copy(out=dy_int[j, g][:, t0 : t0 + 2, :, :], in_=moved[:])
 
         def dy_quant(j, g, t0=0, n=4):
             if t0 == 0:
@@ -286,17 +273,25 @@ def tile_replica_weight_gradient_sketch_s3_kernel(
                 nc.sync.dma_start(out=out[P * i : P * (i + 1), c], in_=res[:, c])
 
         for s in range(4):
-            x0_widen("s" if s > 1 else "v", 0, s)
+            x0_widen("s" if s > 2 else "v", 0, s)
         x0_interleave("v", 0)
-        dy_interleave_by_matmul(0, 0, "bank_a2", 0)
+        dec_t = psum.tile([P, 4, P], BF16, name="bank_a1")
         for t in range(4):
-            dy_interleave("s" if t == 0 else "v", 1, 0, t)
-        dy_interleave_by_matmul(0, 0, "bank_a3", 2)
+            nc.tensor.transpose(dec_t[:, t, :], dec_rows[:, t::4], ident_b[:])
+        zeros_ps = psum.tile([P, K], F32, name="bank_g0")
+        for k in range(WARM):
+            nc.tensor.matmul(
+                out=zeros_ps[:], lhsT=ident_b[:], rhs=x0_int[:, 0:128, :].rearrange("p d s -> p (d s)"), start=True, stop=True
+            )
+        for t in range(4):
+            dy_interleave("s" if t < H0 else "v", 0, 0, t)
+        for t in range(4):
+            dy_interleave("s" if t < H1 else "v", 1, 0, t)
         x0_quant(0)
-        for t in range(4):
-            dy_interleave("s" if t < 2 else "v", 2, 0, t)
         dy_quant(0, 0)
-        nc.vector.tensor_copy(out=dec[:], in_=dec_b[:])
+        nc.vector.tensor_copy(out=dec[:], in_=dec_t[:, :, 0:NG].rearrange("p t g -> p g t"))
+        for t in range(4):
+            dy_interleave("s" if t < HS else "v", 2, 0, t)
         dy_quant(1, 0)
         dy_quant(2, 0, 0, 2)
         dy_quant(2, 0, 2, 2)
@@ -304,7 +299,7 @@ def tile_replica_weight_gradient_sketch_s3_kernel(
         w_transpose(0, 1, "bank_w1")
         decay_times_w(0, 0)
         for s in range(4):
-            x0_widen("s", 1, s)
+            x0_widen(WE, 1, s)
         decay_times_w(0, 1)
 
         units = [(g, i) for g in range(NG) for i in range(ND)]
@@ -327,7 +322,7 @@ def tile_replica_weight_gradient_sketch_s3_kernel(
                 for k in range(12):
                     j, t = divmod(k, 4)
                     if g == 0 and k * 2 // 3 == i or g > 0 and k // 2 == i:
-                        dy_interleave("s" if (t < (3 if j < 1 else 2) if g == 0 else t % 2 == 0 or t == 1 and j < NS) else "v", j, g + 1, t)
+                        dy_interleave("s" if (t < (3, 3, 2)[j] if g == 0 else t % 2 == 0 or t == 1 and j < NS) else "v", j, g + 1, t)
                 if g == 0:
                     if i in (4, 6, 7):
                         dy_quant({4: 0, 6: 1, 7: 2}[i], 1)
@@ -335,7 +330,7 @@ def tile_replica_weight_gradient_sketch_s3_kernel(
                     dy_quant(i // 2 - 1, g + 1)
 
         for n, (g, i) in enumerate(units):
-            gradient(g, i, "g%d" % (n % 2) if n >= 6 else ("g0", "g1", "a2", "a3")[n % 4])
+            gradient(g, i, "g%d" % (n % 3))
             if n == 1:
                 w_transpose(0, 2, "bank_a0")
                 w_transpose(0, 3, "bank_a1")
@@ -358,19 +353,19 @@ def tile_replica_weight_gradient_sketch_s3_kernel(
             add_decay(g, i)
             if n > ND:
                 g_quant(*units[n - 1])
-            if g == 1 and i < 4:
+            if g == 1 and i < EARLY:
                 g_quant(0, i)
-            if g == last and i < 4:
-                g_quant(0, i + 4)
+            if g == last and i < ND - EARLY:
+                g_quant(0, i + EARLY)
             if n > LAG - 1:
                 pg, pi = units[n - LAG]
-                if pi < 4 and pg > 0:
+                if pi < EARLY and pg > 0:
                     for h in range(0 if pg == 1 else pg, pg + 1):
                         project(h, pi, "bank_a%d" % pi)
                     if pg == last:
                         store("s", pi)
         g_quant(*units[-1])
-        for i in range(4, ND):
+        for i in range(EARLY, ND):
             for g in range(NG):
-                project(g, i, "bank_a%d" % (i - 4))
+                project(g, i, "bank_" + ("a0", "a1", "a2", "w0", "w1")[i - EARLY])
             store("s" if i % 2 == 0 else "v", i, 2 if i == ND - 1 else 1)

from contextlib import ExitStack

import concourse.mybir as mybir
from concourse.masks import make_identity

T0, T1, D, F, R = 512, 1024, 1024, 2048, 512
FLOPS = 2 * D * F * (T0 + T1) + 2 * D * F * R

F32 = mybir.dt.float32
BF16 = mybir.dt.bfloat16
U32 = mybir.dt.uint32
I32 = mybir.dt.int32
U8 = mybir.dt.uint8
FP8 = mybir.dt.float8_e4m3fn
FP8X4 = mybir.dt.float8_e4m3fn_x4
FP4X4 = mybir.dt.float4_e2m1fn_x4
COPY = mybir.ActivationFunctionType.Copy
ADD = mybir.AluOpType.add
MULT = mybir.AluOpType.mult

PQ, NS, LAG, EARLY, WARM, HS, H0, H1, WE = 8, 3, 3, 3, 5, 1, 4, 2, "v"
P = 128
K = 512
NJ = (T0 + T1) // K
NG = F // K
ND = D // P


def tile_replica_weight_gradient_sketch_s3_kernel(
    tc, x0_bytes, x0_scale, dy0, x1_words, x1_scales, dy1, w, decay, basis_words, basis_scales, out
):
    nc = tc.nc
    with ExitStack() as ctx:
        keep = ctx.enter_context(tc.tile_pool(name="keep", bufs=1))
        work = ctx.enter_context(tc.tile_pool(name="work", bufs=2))
        psum = ctx.enter_context(tc.psum_pool(name="psum", bufs=1))
        ctx.enter_context(tc.manual_schedule())

        def sb(name, shape, dtype):
            return keep.tile(shape, dtype, name=name, align_bytes=64)

        x0_raw = [sb("x0_raw%d" % h, [P, 4, 512], U8) for h in range(2)]
        x0_sc = sb("x0_sc", [P, 4], F32)
        x0_wide = [sb("x0_wide%d" % h, [P, 4, 512], BF16) for h in range(2)]
        x0_int = sb("x0_int", [P, D, 4], BF16)
        x0_q = sb("x0_q", [P, D], U32)
        x0_s = sb("x0_s", [P, D], U8)
        x1_w = [sb("x1_w%d" % h, [P, 2, D], U8) for h in range(2)]
        x1_s = sb("x1_s", [P, 2, D], U8)
        b_w = sb("b_w", [P, NG, 2 * R], U8)
        b_s = sb("b_s", [P, NG, R], U8)
        dy_raw, w_sb = {}, {}
        for g, n in ((0, 1), (1, 1), (2, 1), (3, 1)):
            for j in range(NJ):
                tile = sb("dy_raw_%d_%d" % (j, g), [P, 4, n * K], BF16)
                for k in range(n):
                    dy_raw[j, g + k] = tile[:, :, K * k : K * (k + 1)]
                dy_raw[j, g, "all"] = tile
            for h in range(2):
                tile = sb("w_sb_%d_%d" % (h, g), [P, 4, n * K], BF16)
                for k in range(n):
                    for i in range(4):
                        w_sb[4 * h + i, g + k] = tile[:, i, K * k : K * (k + 1)]
                w_sb[h, g, "all"] = tile
        dec_rows = sb("dec_rows", [P, K], BF16)
        dec = sb("dec", [P, NG, 4], F32)
        ident = sb("ident", [P, P], F32)
        ident_b = sb("ident_b", [P, P], BF16)
        warm = sb("warm", [P, 1], F32)
        g_q = [sb("g_q%d" % g, [P, D], U32) for g in range(NG)]
        g_s = [sb("g_s%d" % g, [P, D], U8) for g in range(NG)]

        x0_rows = x0_bytes.rearrange("(p s) d -> p s d", s=4)
        dy_rows = [dy0.rearrange("(p s) f -> p s f", s=4)] + [
            dy1[K * j : K * (j + 1), :].rearrange("(p s) f -> p s f", s=4) for j in range(2)
        ]
        w_rows = w.rearrange("(i p) f -> p i f", p=P)
        x1_cols = x1_words.rearrange("g p n -> p g n")

        def load_x0(h):
            c = slice(512 * h, 512 * (h + 1))
            nc.sync.dma_start(out=x0_raw[h][:], in_=x0_rows[:, :, c])

        def load_x1(h):
            c = slice(1024 * h, 1024 * (h + 1))
            nc.sync.dma_start(out=x1_w[h][:], in_=x1_cols[:, :, c])

        def load_dy(j, g, n=1):
            c = slice(K * g, K * (g + n))
            nc.sync.dma_start(out=dy_raw[j, g, "all"][:], in_=dy_rows[j][:, :, c])

        def load_w(h, g, n=1):
            c = slice(K * g, K * (g + n))
            nc.sync.dma_start(out=w_sb[h, g, "all"][:], in_=w_rows[:, 4 * h : 4 * (h + 1), c])

        def load_scales(tile, dram):
            for q in range(4):
                nc.sync.dma_start(
                    out=tile[32 * q : 32 * q + 4, :, :].bitcast(I32),
                    in_=dram[:, 4 * q : 4 * q + 4, :].rearrange("g q n -> q g n").bitcast(I32),
                )

        nc.scalar.dma_start(out=x0_sc[:], in_=x0_scale.rearrange("(p s) o -> p (s o)", s=4))
        nc.vector.memset(x1_s[:].rearrange("p g n -> p (g n)").bitcast(I32), 0)
        nc.vector.memset(dec_rows[:], 0.0)
        make_identity(nc, ident_b[:])
        nc.gpsimd.memset(b_s[:].rearrange("p g n -> p (g n)").bitcast(I32), 0)
        make_identity(nc, ident[:])
        nc.vector.memset(warm[:], 0.0)
        nc.scalar.activation(out=warm[:], in_=warm[:], func=COPY, scale=1.0)

        load_x0(0)
        load_dy(0, 0)
        nc.scalar.dma_start(out=dec_rows[0:NG, :], in_=decay.rearrange("(g k) -> g k", k=K))
        load_dy(1, 0)
        load_dy(2, 0)
        load_scales(x1_s, x1_scales)
        load_w(0, 0)
        load_x1(0)
        load_x0(1)
        load_w(1, 0)
        load_x1(1)
        for j in range(NJ):
            load_dy(j, 1)
        load_w(0, 1)
        nc.sync.dma_start(out=b_w[:], in_=basis_words.rearrange("g p n -> p g n"))
        load_scales(b_s, basis_scales)
        load_w(1, 1)
        for g in (2, 3):
            load_dy(0, g)
            load_dy(1, g)
            load_w(0, g)
            load_dy(2, g)
            load_w(1, g)

        dy_int, dy_q, dy_s = {}, {}, {}

        def copy_on(engine, dst, src):
            if engine == "v":
                nc.vector.tensor_copy(out=dst, in_=src)
            else:
                nc.scalar.copy(out=dst, in_=src)

        def x0_widen(engine, h, s):
            dst, src = x0_wide[h][:, s, :], x0_raw[h][:, s, :].bitcast(FP8)
            if engine == "v":
                nc.vector.tensor_scalar(out=dst, in0=src, scalar1=x0_sc[:, s : s + 1], scalar2=None, op0=MULT)
            else:
                nc.scalar.activation(out=dst, in_=src, func=COPY, scale=x0_sc[:, s : s + 1])

        def x0_interleave(engine, c):
            copy_on(
                engine,
                x0_int[:, 256 * c : 256 * (c + 1), :].rearrange("p (b i) s -> p b s i", i=4),
                x0_wide[c // 2][:, :, 256 * (c % 2) : 256 * (c % 2 + 1)].rearrange("p s (b i) -> p b s i", i=4),
            )

        def x0_quant(c):
            c = slice(256 * c, 256 * (c + 1))
            nc.vector.quantize_mx(
                out=x0_q[:, c].bitcast(FP8X4), scales=x0_s[:, c], in_=x0_int[:, c, :].rearrange("p d s -> p (d s)")
            )

        def dy_interleave(engine, j, g, t):
            if (j, g) not in dy_int:
                dy_int[j, g] = work.tile([P, 4, P, 4], BF16, name="dy_int", bufs=3, align_bytes=64)
            copy_on(
                engine,
                dy_int[j, g][:, t, :, :].rearrange("p (b i) s -> p b s i", i=2),
                dy_raw[j, g].rearrange("p s (b i t) -> p t b s i", i=2, t=4)[:, t],
            )

        def dy_quant(j, g, t0=0, n=4):
            if t0 == 0:
                dy_q[j, g] = work.tile([P, K], U32, name="dy_q%d" % j, align_bytes=64)
                dy_s[j, g] = work.tile([P, K], U8, name="dy_s%d" % j, align_bytes=64)
            c = slice(P * t0, P * (t0 + n))
            nc.vector.quantize_mx(
                out=dy_q[j, g][:, c].bitcast(FP8X4),
                scales=dy_s[j, g][:, c],
                in_=dy_int[j, g][:, t0 : t0 + n, :, :].rearrange("p t m s -> p (t m s)"),
            )

        wt, dw, acc, g_ps, g_in = {}, {}, {}, {}, {}

        w_perm = {}

        def w_permute(g, ip):
            w_perm[g, ip] = work.tile([P, 2, 2, P], F32, name="w_perm", bufs=4, align_bytes=64)
            for half in range(2):
                nc.vector.tensor_copy(
                    out=w_perm[g, ip][:, half, :, :],
                    in_=w_sb[2 * ip + half, g].bitcast(F32).rearrange("p (m u) -> p u m", u=2),
                )

        def w_transpose(g, ip, bank):
            wt[g, ip] = psum.tile([P, 2, 256], F32, name=bank)
            for half in range(2):
                words = w_sb[2 * ip + half, g].bitcast(F32)
                for u in range(2):
                    src = w_perm[g, ip][:, half, u, :] if (g, ip) in w_perm else words[:, u::2]
                    nc.tensor.transpose(wt[g, ip][:, u, P * half : P * (half + 1)], src, ident[:])

        def decay_times_w(g, ip):
            dw[g, ip] = work.tile([P, 4, 256], F32, name="dw", bufs=5, align_bytes=64)
            for t in range(4):
                nc.scalar.activation(
                    out=dw[g, ip][:, t, :],
                    in_=wt[g, ip][:, t // 2, :].bitcast(BF16).rearrange("p (d e) -> p e d", e=2)[:, t % 2, :],
                    func=COPY,
                    scale=dec[:, g, t : t + 1],
                )

        def gradient(g, i, bank):
            g_ps[g, i] = psum.tile([P, 4, P], F32, name="bank_" + bank)
            for t in range(4):
                for j in range(NJ):
                    m = slice(P * t, P * (t + 1))
                    d = slice(P * i, P * (i + 1))
                    if j == 0:
                        rhs, rhs_scale = x0_q[:, d].bitcast(FP8X4), x0_s[:, d]
                    else:
                        rhs = x1_w[i // 4][:, j - 1, 2 * P * (i % 4) : 2 * P * (i % 4 + 1)].bitcast(FP4X4)
                        rhs_scale = x1_s[:, j - 1, d]
                    nc.tensor.matmul_mx(
                        out=g_ps[g, i][:, t, :],
                        lhsT=dy_q[j, g][:, m].bitcast(FP8X4),
                        lhsT_scale=dy_s[j, g][:, m],
                        rhs=rhs,
                        rhs_scale=rhs_scale,
                        start=(j == 0),
                        stop=(j == NJ - 1),
                    )

        def add_decay(g, i):
            if g == 0:
                g_in[g, i] = work.tile([P, P, 4], BF16, name="g_in0", bufs=ND, align_bytes=64)
            else:
                g_in[g, i] = work.tile([P, P, 4], BF16, name="g_in", bufs=4, align_bytes=64)
            half = slice(P * (i % 2), P * (i % 2 + 1))
            nc.vector.tensor_tensor(
                out=g_in[g, i][:].rearrange("p (b i) t -> p b t i", i=2),
                in0=g_ps[g, i][:].rearrange("p t (b i) -> p b t i", i=2),
                in1=dw[g, i // 2][:, :, half].rearrange("p t (b i) -> p b t i", i=2),
                op=ADD,
            )

        def g_quant(g, i):
            d = slice(P * i, P * (i + 1))
            nc.vector.quantize_mx(
                out=g_q[g][:, d].bitcast(FP8X4), scales=g_s[g][:, d], in_=g_in[g, i][:].rearrange("p d t -> p (d t)")
            )

        def project(g, i, bank):
            if i not in acc:
                acc[i] = psum.tile([P, R], F32, name=bank)
            d = slice(P * i, P * (i + 1))
            nc.tensor.matmul_mx(
                out=acc[i][:],
                lhsT=g_q[g][:, d].bitcast(FP8X4),
                lhsT_scale=g_s[g][:, d],
                rhs=b_w[:, g, :].bitcast(FP4X4),
                rhs_scale=b_s[:, g, :],
                start=(g == 0),
                stop=(g == NG - 1),
            )

        def store(engine, i, pieces=1):
            res = work.tile([P, R], F32, name="res", bufs=6, align_bytes=64)
            for k in range(pieces):
                c = slice(R * k // pieces, R * (k + 1) // pieces)
                copy_on(engine, res[:, c], acc[i][:, c])
                nc.sync.dma_start(out=out[P * i : P * (i + 1), c], in_=res[:, c])

        for s in range(4):
            x0_widen("s" if s > 2 else "v", 0, s)
        x0_interleave("v", 0)
        dec_t = psum.tile([P, 4, P], BF16, name="bank_a1")
        for t in range(4):
            nc.tensor.transpose(dec_t[:, t, :], dec_rows[:, t::4], ident_b[:])
        zeros_ps = psum.tile([P, K], F32, name="bank_g0")
        for k in range(WARM):
            nc.tensor.matmul(
                out=zeros_ps[:], lhsT=ident_b[:], rhs=x0_int[:, 0:128, :].rearrange("p d s -> p (d s)"), start=True, stop=True
            )
        for t in range(4):
            dy_interleave("s" if t < H0 else "v", 0, 0, t)
        for t in range(4):
            dy_interleave("s" if t < H1 else "v", 1, 0, t)
        x0_quant(0)
        dy_quant(0, 0)
        nc.vector.tensor_copy(out=dec[:], in_=dec_t[:, :, 0:NG].rearrange("p t g -> p g t"))
        for t in range(4):
            dy_interleave("s" if t < HS else "v", 2, 0, t)
        dy_quant(1, 0)
        dy_quant(2, 0, 0, 2)
        dy_quant(2, 0, 2, 2)
        w_transpose(0, 0, "bank_w0")
        w_transpose(0, 1, "bank_w1")
        decay_times_w(0, 0)
        for s in range(4):
            x0_widen(WE, 1, s)
        decay_times_w(0, 1)

        units = [(g, i) for g in range(NG) for i in range(ND)]
        last = NG - 1

        def prepare(g, i):
            if g == 0:
                if i == 0:
                    x0_interleave("v", 1)
                elif i == 1:
                    x0_quant(1)
                elif i == 2:
                    x0_interleave("v", 2)
                elif i == 3:
                    x0_quant(2)
                    x0_interleave("v", 3)
                elif i == 4:
                    x0_quant(3)
            if g < last:
                for k in range(12):
                    j, t = divmod(k, 4)
                    if g == 0 and k * 2 // 3 == i or g > 0 and k // 2 == i:
                        dy_interleave("s" if (t < (3, 3, 2)[j] if g == 0 else t % 2 == 0 or t == 1 and j < NS) else "v", j, g + 1, t)
                if g == 0:
                    if i in (4, 6, 7):
                        dy_quant({4: 0, 6: 1, 7: 2}[i], 1)
                elif i in (2, 4, 6):
                    dy_quant(i // 2 - 1, g + 1)

        for n, (g, i) in enumerate(units):
            gradient(g, i, "g%d" % (n % 3))
            if n == 1:
                w_transpose(0, 2, "bank_a0")
                w_transpose(0, 3, "bank_a1")
            elif n == 5:
                w_transpose(1, 0, "bank_w0")
                w_transpose(1, 1, "bank_w1")
            elif n == 8:
                w_transpose(1, 2, "bank_a0")
                w_transpose(1, 3, "bank_a1")
            if n % 4 >= 2 and PQ <= n // 4 * 2 + 2 + n % 4 < 16:
                q = n // 4 * 2 + 2 + n % 4
                w_permute(q // 4, q % 4)
            if n > 9 and n % 4 == 0 and n < 27:
                for q in (n // 2 + 2, n // 2 + 3):
                    w_transpose(q // 4, q % 4, "bank_w%d" % (q % 2))
            prepare(g, i)
            for q in range(2, 4 * NG):
                if n == {4: 6, 5: 8}.get(q, 2 * q - 3):
                    decay_times_w(q // 4, q % 4)
            add_decay(g, i)
            if n > ND:
                g_quant(*units[n - 1])
            if g == 1 and i < EARLY:
                g_quant(0, i)
            if g == last and i < ND - EARLY:
                g_quant(0, i + EARLY)
            if n > LAG - 1:
                pg, pi = units[n - LAG]
                if pi < EARLY and pg > 0:
                    for h in range(0 if pg == 1 else pg, pg + 1):
                        project(h, pi, "bank_a%d" % pi)
                    if pg == last:
                        store("s", pi)
        g_quant(*units[-1])
        for i in range(EARLY, ND):
            for g in range(NG):
                project(g, i, "bank_" + ("a0", "a1", "a2", "w0", "w1")[i - EARLY])
            store("s" if i % 2 == 0 else "v", i, 2 if i == ND - 1 else 1)
